import numpy as np
import ml_dtypes


def mxq(x, axis, fmt="e4m3"):
    dtype, down = {"e4m3": (ml_dtypes.float8_e4m3fn, 7), "e5m2": (ml_dtypes.float8_e5m2, 14)}[fmt]
    v = np.moveaxis(np.asarray(x, np.float32).astype(ml_dtypes.bfloat16).astype(np.float64), axis, -1)
    blocks = v.reshape(v.shape[:-1] + (-1, 32))
    amax = np.abs(blocks).max(-1, keepdims=True)
    byte = np.maximum(np.where(amax > 0, np.frexp(amax)[1] - 1 + 127, 0) - down, 1)
    scale = np.exp2(byte - 127.0)
    codes = (blocks / scale).astype(np.float32).astype(dtype).astype(np.float64)
    return np.moveaxis((codes * scale).reshape(v.shape), -1, axis)


WIDE = False


def mx_kscale(k):
    if not WIDE:
        return np.ones(k)
    levels = np.array([10, -10, 5, -5, 0])
    if k % 512:
        return np.exp2(np.random.permutation(np.resize(levels, k // 32))).repeat(32)
    a = np.empty((k // 512, 16))
    for p in range(k // 512):
        a[p, :8] = np.random.permutation(np.resize(levels, 8))
        for g in range(8):
            far = levels[np.abs(levels - a[p, g]) >= 10]
            a[p, g + 8] = far[np.random.randint(len(far))]
    return np.exp2(a.ravel()).repeat(32)


def f64(x):
    return np.asarray(x).astype(np.float64)


def striped(idx):
    return np.tile(idx.reshape(-1, 16).T, (8, 1)).astype(np.uint16)


def unstriped(offs):
    return offs[:16].T.reshape(-1).astype(np.int64)


def pack_weight(w):
    k, n = w.shape
    w = f64(np.asarray(w, np.float32).astype(ml_dtypes.bfloat16)).reshape(k // 32, 32, n)
    amax = np.abs(w).max(1)
    byte = np.clip(np.where(amax > 0, np.frexp(amax)[1] - 1 + 127 - 7, 1), 1, 254)
    scaled = (w * np.exp2(127.0 - byte)[:, None, :]).reshape(k, n).astype(np.float32)
    words = np.ascontiguousarray(scaled.reshape(k // 512, 128, 4, n).transpose(0, 1, 3, 2)).astype(ml_dtypes.float8_e4m3fn).view(np.uint8)
    return words, np.ascontiguousarray(byte.astype(np.uint8).reshape(k // 512, 16, n))


def unpack_weight(words, scales):
    g, p, n, _ = words.shape
    vals = np.ascontiguousarray(words).view(ml_dtypes.float8_e4m3fn).astype(np.float64) * np.repeat(np.exp2(scales.astype(np.float64) - 127.0), 8, axis=1)[..., None]
    return vals.transpose(0, 1, 3, 2).reshape(g * 512, n)


def relu(v):
    return np.maximum(v, 0.0)

def planes(y):
    n, m = y.shape
    v = y.astype(np.float32).astype(ml_dtypes.bfloat16).astype(np.float64).reshape(n // 32, 32, m)
    top = np.abs(v).max(1)
    byte = np.clip(np.where(top > 0, np.frexp(top)[1] - 1 + 127 - 7, 1), 1, 254)
    codes = (v * np.exp2(127.0 - byte)[:, None, :]).reshape(n, m).astype(np.float32).astype(ml_dtypes.float8_e4m3fn).view(np.uint8)
    words = codes.reshape(n // 512, 128, 4, m).transpose(0, 1, 3, 2)
    return np.ascontiguousarray(words), np.ascontiguousarray(byte.astype(np.uint8).reshape(n // 512, 16, m))


K, T, S, H, U, V = 512, 2048, 1024, 512, 1024, 512


def setup_inputs():
    n = np.random.standard_normal
    s = mx_kscale(K)[:, None]
    u = mx_kscale(H)
    packed_xT = pack_weight(n((K, T)) * s)
    packed_w3 = pack_weight(n((H, H)) / np.sqrt(H) / u[:, None])
    return {
        "x_words": packed_xT[0],
        "x_scales": packed_xT[1],
        "w1": (n((K, H)) / np.sqrt(K) / s * u).astype(np.float32),
        "w2": (n((K, H)) / np.sqrt(K) / s * u).astype(np.float32),
        "w3_words": packed_w3[0],
        "w3_scales": packed_w3[1],
        "offs": striped(np.random.permutation(T)[:S]),
        "near": striped(np.random.permutation(U)[:V]),
        "far": striped(np.random.permutation(U)[:V]),
    }


def reference(x_words, x_scales, w1, w2, w3_words, w3_scales, offs, near, far):
    xq = unpack_weight(x_words, x_scales)[:, unstriped(offs)]
    a = np.zeros((H, S))
    a[:, unstriped(near)] = relu(mxq(f64(w1), 0, "e4m3").T @ xq[:, :V])
    e = np.zeros((H, S))
    e[:, unstriped(far)] = relu(mxq(f64(w2), 0, "e4m3").T @ xq[:, V:2 * V])
    z = np.maximum(a, e)
    out_0 = unpack_weight(w3_words, w3_scales).T @ mxq(z, 0, "e4m3")
    return (out_0,) + planes(out_0)

@@ -1,0 +1,223 @@
+from contextlib import ExitStack
+
+import concourse.mybir as mybir
+
+K, T, S, H, U, V = 512, 2048, 1024, 512, 1024, 512
+FLOPS = 2 * K * H * S + 2 * H * H * U
+
+F32 = mybir.dt.float32
+BF16 = mybir.dt.bfloat16
+I32 = mybir.dt.int32
+U32 = mybir.dt.uint32
+U16 = mybir.dt.uint16
+U8 = mybir.dt.uint8
+FP8X4 = mybir.dt.float8_e4m3fn_x4
+ACT = mybir.ActivationFunctionType
+ALU = mybir.AluOpType
+
+P = 128
+PACK = 4
+QUADS = 4
+LANE = 16
+CHUNK = 256
+CHUNKS = U // CHUNK
+RUN = 4
+HALF = 256
+SHARE = 128
+
+
+def tile_picked_bev_max_po_kernel(
+    tc, x_words, x_scales, w1, w2, w3_words, w3_scales, offs, near, far, out_0, out_1, out_2
+):
+    nc = tc.nc
+    with ExitStack() as ctx:
+        keep = ctx.enter_context(tc.tile_pool(name="keep", bufs=1))
+        psum = ctx.enter_context(tc.psum_pool(name="psum", bufs=8))
+
+        def tiles(name, count, shape, dtype):
+            return [keep.tile(shape, dtype, name="%s%d" % (name, i), align_bytes=64) for i in range(count)]
+
+        offs_t = keep.tile([P, S // LANE], U16)
+        near_t = keep.tile([P, V // LANE], U16)
+        far_t = keep.tile([P, V // LANE], U16)
+        lists = [near_t, far_t]
+
+        x_table = keep.tile([P, T], I32, align_bytes=64)
+        x_bytes = keep.tile([P, T], U8, align_bytes=64)
+        w_raw = tiles("w_raw", 2, [P, PACK, H], F32)
+        w_dealt = tiles("w_dealt", 2, [P, H * PACK], BF16)
+        w_codes = tiles("w_codes", 2, [P, H], U32)
+        w_scales = tiles("w_scales", 2, [P, H], U8)
+        w3_raw = keep.tile([P, H], I32, align_bytes=64)
+        w3_raw_bytes = keep.tile([P, H], U8, align_bytes=64)
+        w3_codes = keep.tile([P, H], U32, align_bytes=64)
+        w3_bytes = keep.tile([P, H], U8, align_bytes=64)
+        picked_words = tiles("picked_words", 2, [P, V], U32)
+        picked_bytes = tiles("picked_bytes", 2, [P, V], U8)
+        hidden = [tiles("hidden%d_" % s, PACK, [P, V], F32) for s in range(2)]
+        cells = [tiles("cells%d_" % s, PACK, [P, U], F32) for s in range(2)]
+        z_rows = keep.tile([P, CHUNKS, PACK, CHUNK], BF16, align_bytes=64)
+        z_woven = tiles("z_woven", CHUNKS, [P, CHUNK, PACK], BF16)
+        z_codes = tiles("z_codes", CHUNKS, [P, CHUNK], U32)
+        z_scales = tiles("z_scales", CHUNKS, [P, CHUNK], U8)
+        y_rows = tiles("y_rows", CHUNKS, [P, PACK, CHUNK], F32)
+        y_woven = tiles("y_woven", CHUNKS, [P, CHUNK, PACK], BF16)
+        y_codes = tiles("y_codes", CHUNKS, [P, CHUNK], U32)
+        y_scales = keep.tile([P, U], U8, align_bytes=64)
+
+        def load_scale_rows(queue, plane, rows):
+            for q in range(QUADS):
+                queue.dma_start(out=plane[32 * q : 32 * q + 4, :].bitcast(I32), in_=rows[4 * q : 4 * q + 4, :].bitcast(I32))
+
+        nc.vector.memset(x_bytes[:].bitcast(I32), 0)
+        nc.vector.memset(w3_raw_bytes[:].bitcast(I32), 0)
+
+        nc.sync.dma_start(out=w_raw[0][:], in_=w1.rearrange("(p j) c -> p j c", j=PACK))
+        load_scale_rows(nc.sync, x_bytes, x_scales[0])
+        nc.sync.dma_start(offs_t[:], offs)
+        nc.sync.dma_start(out=x_table[:], in_=x_words[0].rearrange("p n r -> p (n r)").bitcast(I32))
+        nc.sync.dma_start(near_t[:], near)
+        nc.sync.dma_start(out=w_raw[1][:], in_=w2.rearrange("(p j) c -> p j c", j=PACK))
+        nc.sync.dma_start(far_t[:], far)
+        nc.sync.dma_start(out=w3_raw[:], in_=w3_words[0].rearrange("p n r -> p (n r)").bitcast(I32))
+        load_scale_rows(nc.sync, w3_raw_bytes, w3_scales[0])
+
+        for s in range(2):
+            for t in range(PACK):
+                nc.vector.memset(cells[s][t][:].bitcast(I32), 0)
+
+        def deal_views(s):
+            dst = w_dealt[s][:].rearrange("p (t m j) -> p m j t", t=PACK, j=PACK)
+            src = w_raw[s][:].rearrange("p j (m t) -> p m j t", t=PACK)
+            return dst, src
+
+        def picked(table, s):
+            return table.indirect(offs_t[:, s * V // LANE : (s + 1) * V // LANE])
+
+        def quantize(codes, scales, values):
+            nc.vector.quantize_mx(out=codes.bitcast(FP8X4), scales=scales, in_=values)
+
+        def first_products(s):
+            banks = []
+            for t in range(PACK):
+                bank = psum.tile([P, V], F32, name="bank")
+                cols = slice(t * P, (t + 1) * P)
+                nc.tensor.matmul_mx(
+                    out=bank[:],
+                    lhsT=w_codes[s][:, cols].bitcast(FP8X4),
+                    lhsT_scale=w_scales[s][:, cols],
+                    rhs=picked_words[s][:].bitcast(FP8X4),
+                    rhs_scale=picked_bytes[s][:],
+                    start=True,
+                    stop=True,
+                )
+                banks.append(bank)
+            return banks
+
+        def relu_scalar(s, t, bank):
+            nc.scalar.activation(out=hidden[s][t][:], in_=bank[:], func=ACT.Relu)
+
+        def relu_vector(s, t, bank):
+            nc.vector.tensor_scalar_max(out=hidden[s][t][:], in0=bank[:], scalar1=0.0)
+
+        def scatter_vector(s, t, lo, hi):
+            window = cells[s][t][:].indirect(lists[s][:, lo // LANE : hi // LANE])
+            nc.vector.tensor_copy(out=window, in_=hidden[s][t][:, lo:hi])
+
+        def scatter_scalar(s, t, lo, hi):
+            for a in range(lo, hi, 384 if hi - lo == 384 else HALF):
+                b = min(hi, a + (384 if hi - lo == 384 else HALF))
+                window = cells[s][t][:].indirect(lists[s][:, a // LANE : b // LANE])
+                nc.scalar.activation(out=window, in_=hidden[s][t][:, a:b], func=ACT.Copy)
+
+        def join(t, c0, c1):
+            cols = slice(c0 * CHUNK, c1 * CHUNK)
+            nc.vector.tensor_tensor(
+                out=z_rows[:, c0:c1, t, :],
+                in0=cells[0][t][:, cols].rearrange("p (k c) -> p k c", c=CHUNK),
+                in1=cells[1][t][:, cols].rearrange("p (k c) -> p k c", c=CHUNK),
+                op=ALU.max,
+            )
+
+        def weave(copy, woven, rows):
+            copy(out=woven.rearrange("p (c i) t -> p c t i", i=RUN), in_=rows.rearrange("p t (c i) -> p c t i", i=RUN))
+
+        dst, src = deal_views(0)
+        nc.scalar.activation(out=dst, in_=src, func=ACT.Copy)
+        nc.vector.tensor_copy(out=picked_bytes[0][:], in_=picked(x_bytes[:], 0))
+        quantize(w_codes[0][:], w_scales[0][:], w_dealt[0][:])
+        nc.vector.tensor_copy(out=picked_words[0][:], in_=picked(x_table[:].bitcast(U32), 0))
+        banks = first_products(0)
+        for t in range(PACK):
+            relu_scalar(0, t, banks[t])
+        nc.vector.tensor_copy(out=picked_words[1][:], in_=picked(x_table[:].bitcast(U32), 1))
+        nc.vector.tensor_copy(out=picked_bytes[1][:], in_=picked(x_bytes[:], 1))
+        scatter_vector(0, 0, 0, V)
+        scatter_vector(0, 3, 0, SHARE)
+        scatter_scalar(0, 1, 0, V)
+        scatter_scalar(0, 2, 0, V)
+        scatter_scalar(0, 3, SHARE, V)
+
+        dst, src = deal_views(1)
+        nc.vector.tensor_copy(out=dst, in_=src)
+        nc.vector.tensor_copy(
+            out=w3_codes[:].rearrange("p (t m) -> p m t", t=PACK),
+            in_=w3_raw[:].bitcast(U32).rearrange("p (m t) -> p m t", t=PACK),
+        )
+        quantize(w_codes[1][:], w_scales[1][:], w_dealt[1][:])
+        nc.vector.tensor_copy(
+            out=w3_bytes[:].rearrange("p (t m) -> p m t", t=PACK),
+            in_=w3_raw_bytes[:].rearrange("p (m t) -> p m t", t=PACK),
+        )
+        banks = first_products(1)
+        for t in range(2):
+            relu_vector(1, t, banks[t])
+            scatter_vector(1, t, 0, V)
+            join(t, 0, CHUNKS)
+        for t in range(2, PACK):
+            relu_scalar(1, t, banks[t])
+            scatter_scalar(1, t, 0, V)
+        join(2, 0, CHUNKS)
+
+        out_rows = out_0.rearrange("(p t) r -> p t r", t=PACK)
+        out_words = out_1[0].rearrange("p n r -> p (n r)").bitcast(I32)
+
+        def z_front(c):
+            join(3, c, c + 1)
+            weave(nc.scalar.copy if c % 2 else nc.vector.tensor_copy, z_woven[c][:], z_rows[:, c, :, :])
+
+        def z_product(c):
+            quantize(z_codes[c][:], z_scales[c][:], z_woven[c][:].rearrange("p c t -> p (c t)"))
+            for pair in range(2):
+                bank = psum.tile([P, 2, CHUNK], F32, name="bank")
+                for u in range(2):
+                    cols = slice((2 * pair + u) * P, (2 * pair + u + 1) * P)
+                    nc.tensor.matmul_mx(
+                        out=bank[:, u, :],
+                        lhsT=w3_codes[:, cols].bitcast(FP8X4),
+                        lhsT_scale=w3_bytes[:, cols],
+                        rhs=z_codes[c][:].bitcast(FP8X4),
+                        rhs_scale=z_scales[c][:],
+                        start=True,
+                        stop=True,
+                    )
+                nc.scalar.copy(out=y_rows[c][:, 2 * pair : 2 * pair + 2, :], in_=bank[:])
+            nc.sync.dma_start(out=out_rows[:, :, c * CHUNK : (c + 1) * CHUNK], in_=y_rows[c][:])
+
+        def y_weave(c):
+            weave(nc.vector.tensor_copy, y_woven[c][:], y_rows[c][:])
+
+        def y_planes(c):
+            cols = slice(c * CHUNK, (c + 1) * CHUNK)
+            quantize(y_codes[c][:], y_scales[:, cols], y_woven[c][:].rearrange("p c t -> p (c t)"))
+            nc.sync.dma_start(out=out_words[:, cols], in_=y_codes[c][:].bitcast(I32))
+
+        stages = [z_front, z_product, y_weave, y_planes]
+        for step in range(CHUNKS + len(stages) - 1):
+            for lag, stage in enumerate(stages):
+                if 0 <= step - lag < CHUNKS:
+                    stage(step - lag)
+
+        for q in range(QUADS):
+            queue = nc.scalar if q % 2 else nc.sync
+            queue.dma_start(out=out_2[0][4 * q : 4 * q + 4, :].bitcast(I32), in_=y_scales[32 * q : 32 * q + 4, :].bitcast(I32))

@@ -19,8 +19,12 @@ P = 128
 PACK = 4
 QUADS = 4
 LANE = 16
-CHUNK = 256
-CHUNKS = U // CHUNK
+UNIT = 128
+UNITS = U // UNIT
+WIDTHS = [128,256,256,256,128]
+CHUNKS = len(WIDTHS)
+STARTS = [sum(WIDTHS[:c]) for c in range(CHUNKS)]
+BANK = 512
 RUN = 4
 HALF = 256
 SHARE = 128
@@ -56,13 +60,17 @@ def tile_picked_bev_max_po_kernel(
         picked_bytes = tiles("picked_bytes", 2, [P, V], U8)
         hidden = [tiles("hidden%d_" % s, PACK, [P, V], F32) for s in range(2)]
         cells = [tiles("cells%d_" % s, PACK, [P, U], F32) for s in range(2)]
-        z_rows = keep.tile([P, CHUNKS, PACK, CHUNK], BF16, align_bytes=64)
-        z_woven = tiles("z_woven", CHUNKS, [P, CHUNK, PACK], BF16)
-        z_codes = tiles("z_codes", CHUNKS, [P, CHUNK], U32)
-        z_scales = tiles("z_scales", CHUNKS, [P, CHUNK], U8)
-        y_rows = tiles("y_rows", CHUNKS, [P, PACK, CHUNK], F32)
-        y_woven = tiles("y_woven", CHUNKS, [P, CHUNK, PACK], BF16)
-        y_codes = tiles("y_codes", CHUNKS, [P, CHUNK], U32)
+        z_rows = keep.tile([P, UNITS, PACK, UNIT], BF16, align_bytes=64)
+
+        def chunk_tiles(name, shape, dtype):
+            return [keep.tile(shape(w), dtype, name="%s%d" % (name, c), align_bytes=64) for c, w in enumerate(WIDTHS)]
+
+        z_woven = chunk_tiles("z_woven", lambda w: [P, w, PACK], BF16)
+        z_codes = chunk_tiles("z_codes", lambda w: [P, w], U32)
+        z_scales = chunk_tiles("z_scales", lambda w: [P, w], U8)
+        y_rows = chunk_tiles("y_rows", lambda w: [P, PACK, w], F32)
+        y_woven = chunk_tiles("y_woven", lambda w: [P, w, PACK], BF16)
+        y_codes = keep.tile([P, U], U32, align_bytes=64)
         y_scales = keep.tile([P, U], U8, align_bytes=64)
 
         def load_scale_rows(queue, plane, rows):
@@ -70,7 +78,7 @@ def tile_picked_bev_max_po_kernel(
                 queue.dma_start(out=plane[32 * q : 32 * q + 4, :].bitcast(I32), in_=rows[4 * q : 4 * q + 4, :].bitcast(I32))
 
         nc.vector.memset(x_bytes[:].bitcast(I32), 0)
-        nc.vector.memset(w3_raw_bytes[:].bitcast(I32), 0)
+        nc.gpsimd.memset(w3_raw_bytes[:].bitcast(I32), 0)
 
         nc.sync.dma_start(out=w_raw[0][:], in_=w1.rearrange("(p j) c -> p j c", j=PACK))
         load_scale_rows(nc.sync, x_bytes, x_scales[0])
@@ -84,7 +92,8 @@ def tile_picked_bev_max_po_kernel(
 
         for s in range(2):
             for t in range(PACK):
-                nc.vector.memset(cells[s][t][:].bitcast(I32), 0)
+                engine = nc.vector if s == 0 and t < 3 else nc.gpsimd
+                engine.memset(cells[s][t][:], 0.0)
 
         def deal_views(s):
             dst = w_dealt[s][:].rearrange("p (t m j) -> p m j t", t=PACK, j=PACK)
@@ -130,17 +139,13 @@ def tile_picked_bev_max_po_kernel(
                 window = cells[s][t][:].indirect(lists[s][:, a // LANE : b // LANE])
                 nc.scalar.activation(out=window, in_=hidden[s][t][:, a:b], func=ACT.Copy)
 
-        def join(t, c0, c1):
-            cols = slice(c0 * CHUNK, c1 * CHUNK)
+        def join(t, lo, hi):
             nc.vector.tensor_tensor(
-                out=z_rows[:, c0:c1, t, :],
-                in0=cells[0][t][:, cols].rearrange("p (k c) -> p k c", c=CHUNK),
-                in1=cells[1][t][:, cols].rearrange("p (k c) -> p k c", c=CHUNK),
+                out=z_rows[:, lo // UNIT : hi // UNIT, t, :],
+                in0=cells[0][t][:, lo:hi].rearrange("p (u c) -> p u c", c=UNIT),
+                in1=cells[1][t][:, lo:hi].rearrange("p (u c) -> p u c", c=UNIT),
                 op=ALU.max,
             )
-
-        def weave(copy, woven, rows):
-            copy(out=woven.rearrange("p (c i) t -> p c t i", i=RUN), in_=rows.rearrange("p t (c i) -> p c t i", i=RUN))
 
         dst, src = deal_views(0)
         nc.scalar.activation(out=dst, in_=src, func=ACT.Copy)
@@ -173,50 +178,86 @@ def tile_picked_bev_max_po_kernel(
         for t in range(2):
             relu_vector(1, t, banks[t])
             scatter_vector(1, t, 0, V)
-            join(t, 0, CHUNKS)
+            join(t, 0, U)
         for t in range(2, PACK):
             relu_scalar(1, t, banks[t])
             scatter_scalar(1, t, 0, V)
-        join(2, 0, CHUNKS)
+        join(2, 0, U)
 
         out_rows = out_0.rearrange("(p t) r -> p t r", t=PACK)
         out_words = out_1[0].rearrange("p n r -> p (n r)").bitcast(I32)
 
-        def z_front(c):
-            join(3, c, c + 1)
-            weave(nc.scalar.copy if c % 2 else nc.vector.tensor_copy, z_woven[c][:], z_rows[:, c, :, :])
+        def z_join(c):
+            join(3, STARTS[c], STARTS[c] + WIDTHS[c])
+
+        def z_weave(c, copy):
+            rows = z_rows[:, STARTS[c] // UNIT : (STARTS[c] + WIDTHS[c]) // UNIT, :, :]
+            copy(
+                out=z_woven[c][:].rearrange("p (u c i) t -> p u c t i", c=UNIT // RUN, i=RUN),
+                in_=rows.rearrange("p u t (c i) -> p u c t i", i=RUN),
+            )
 
         def z_product(c):
+            width = WIDTHS[c]
+            cols = slice(STARTS[c], STARTS[c] + width)
             quantize(z_codes[c][:], z_scales[c][:], z_woven[c][:].rearrange("p c t -> p (c t)"))
-            for pair in range(2):
-                bank = psum.tile([P, 2, CHUNK], F32, name="bank")
-                for u in range(2):
-                    cols = slice((2 * pair + u) * P, (2 * pair + u + 1) * P)
+            per_bank = BANK // width
+            for t0 in range(0, PACK, per_bank):
+                bank = psum.tile([P, per_bank, width], F32, name="bank")
+                for u in range(per_bank):
+                    rows = slice((t0 + u) * P, (t0 + u + 1) * P)
                     nc.tensor.matmul_mx(
                         out=bank[:, u, :],
-                        lhsT=w3_codes[:, cols].bitcast(FP8X4),
-                        lhsT_scale=w3_bytes[:, cols],
+                        lhsT=w3_codes[:, rows].bitcast(FP8X4),
+                        lhsT_scale=w3_bytes[:, rows],
                         rhs=z_codes[c][:].bitcast(FP8X4),
                         rhs_scale=z_scales[c][:],
                         start=True,
                         stop=True,
                     )
-                nc.scalar.copy(out=y_rows[c][:, 2 * pair : 2 * pair + 2, :], in_=bank[:])
-            nc.sync.dma_start(out=out_rows[:, :, c * CHUNK : (c + 1) * CHUNK], in_=y_rows[c][:])
+                nc.scalar.copy(out=y_rows[c][:, t0 : t0 + per_bank, :], in_=bank[:])
+            nc.sync.dma_start(out=out_rows[:, :, cols], in_=y_rows[c][:])
 
-        def y_weave(c):
-            weave(nc.vector.tensor_copy, y_woven[c][:], y_rows[c][:])
+        def y_weave(c, copy):
+            copy(
+                out=y_woven[c][:].rearrange("p (c i) t -> p c t i", i=RUN),
+                in_=y_rows[c][:].rearrange("p t (c i) -> p c t i", i=RUN),
+            )
 
         def y_planes(c):
-            cols = slice(c * CHUNK, (c + 1) * CHUNK)
-            quantize(y_codes[c][:], y_scales[:, cols], y_woven[c][:].rearrange("p c t -> p (c t)"))
-            nc.sync.dma_start(out=out_words[:, cols], in_=y_codes[c][:].bitcast(I32))
+            cols = slice(STARTS[c], STARTS[c] + WIDTHS[c])
+            quantize(y_codes[:, cols], y_scales[:, cols], y_woven[c][:].rearrange("p c t -> p (c t)"))
 
-        stages = [z_front, z_product, y_weave, y_planes]
-        for step in range(CHUNKS + len(stages) - 1):
-            for lag, stage in enumerate(stages):
-                if 0 <= step - lag < CHUNKS:
-                    stage(step - lag)
+        def store_words(lo, hi):
+            nc.sync.dma_start(out=out_words[:, lo:hi], in_=y_codes[:, lo:hi].bitcast(I32))
+
+        z_join(0)
+        z_weave(0, nc.vector.tensor_copy)
+        z_join(1)
+        z_weave(1, nc.scalar.copy)
+        z_product(0)
+        y_weave(0, nc.scalar.copy)
+        z_join(2)
+        z_weave(2, nc.vector.tensor_copy)
+        z_join(3)
+        z_product(1)
+        z_product(2)
+        z_weave(3, nc.vector.tensor_copy)
+        z_join(4)
+        z_product(3)
+        z_weave(4, nc.vector.tensor_copy)
+        y_planes(0)
+        z_product(4)
+        y_weave(1, nc.vector.tensor_copy)
+        y_weave(2, nc.vector.tensor_copy)
+        y_planes(1)
+        y_weave(3, nc.vector.tensor_copy)
+        y_planes(2)
+        store_words(0, 640)
+        y_weave(4, nc.scalar.copy)
+        y_planes(3)
+        y_planes(4)
+        store_words(640, U)
 
         for q in range(QUADS):
             queue = nc.scalar if q % 2 else nc.sync

@@ -27,7 +27,7 @@ STARTS = [sum(WIDTHS[:c]) for c in range(CHUNKS)]
 BANK = 512
 RUN = 4
 HALF = 256
-SHARE = 128
+SHARE = 192
 
 
 def tile_picked_bev_max_po_kernel(
@@ -48,17 +48,18 @@ def tile_picked_bev_max_po_kernel(
 
         x_table = keep.tile([P, T], I32, align_bytes=64)
         x_bytes = keep.tile([P, T], U8, align_bytes=64)
-        w_raw = tiles("w_raw", 2, [P, PACK, H], F32)
+        w1_raw = keep.tile([P, PACK, H], F32, align_bytes=64)
+        w2_raw = [keep.tile([P, PACK, H // 2], F32, name="w2_raw%d" % i, tag="w2_raw%d" % i, align_bytes=64) for i in range(2)]
         w_dealt = tiles("w_dealt", 2, [P, H * PACK], BF16)
         w_codes = tiles("w_codes", 2, [P, H], U32)
         w_scales = tiles("w_scales", 2, [P, H], U8)
-        w3_raw = keep.tile([P, H], I32, align_bytes=64)
+        w3_raw = keep.tile([P, H], I32, tag="w3_raw", align_bytes=64)
         w3_raw_bytes = keep.tile([P, H], U8, align_bytes=64)
         w3_codes = keep.tile([P, H], U32, align_bytes=64)
         w3_bytes = keep.tile([P, H], U8, align_bytes=64)
         picked_words = tiles("picked_words", 2, [P, V], U32)
-        picked_bytes = tiles("picked_bytes", 2, [P, V], U8)
-        hidden = [tiles("hidden%d_" % s, PACK, [P, V], F32) for s in range(2)]
+        picked_bytes = []
+        hidden = {}
         cells = [tiles("cells%d_" % s, PACK, [P, U], F32) for s in range(2)]
         z_rows = keep.tile([P, UNITS, PACK, UNIT], BF16, align_bytes=64)
 
@@ -78,26 +79,27 @@ def tile_picked_bev_max_po_kernel(
                 queue.dma_start(out=plane[32 * q : 32 * q + 4, :].bitcast(I32), in_=rows[4 * q : 4 * q + 4, :].bitcast(I32))
 
         nc.vector.memset(x_bytes[:].bitcast(I32), 0)
-        nc.gpsimd.memset(w3_raw_bytes[:].bitcast(I32), 0)
+        nc.vector.memset(w3_raw_bytes[:].bitcast(I32), 0)
 
-        nc.sync.dma_start(out=w_raw[0][:], in_=w1.rearrange("(p j) c -> p j c", j=PACK))
+        nc.sync.dma_start(out=w1_raw[:], in_=w1.rearrange("(p j) c -> p j c", j=PACK))
         load_scale_rows(nc.sync, x_bytes, x_scales[0])
         nc.sync.dma_start(offs_t[:], offs)
         nc.sync.dma_start(out=x_table[:], in_=x_words[0].rearrange("p n r -> p (n r)").bitcast(I32))
         nc.sync.dma_start(near_t[:], near)
-        nc.sync.dma_start(out=w_raw[1][:], in_=w2.rearrange("(p j) c -> p j c", j=PACK))
-        nc.sync.dma_start(far_t[:], far)
+        w2_rows = w2.rearrange("(p j) c -> p j c", j=PACK)
+        nc.sync.dma_start(out=w2_raw[0][:], in_=w2_rows[:, :, : H // 2])
         nc.sync.dma_start(out=w3_raw[:], in_=w3_words[0].rearrange("p n r -> p (n r)").bitcast(I32))
+        nc.sync.dma_start(out=w2_raw[1][:], in_=w2_rows[:, :, H // 2 :])
+        nc.sync.dma_start(far_t[:], far)
         load_scale_rows(nc.sync, w3_raw_bytes, w3_scales[0])
 
         for s in range(2):
             for t in range(PACK):
-                engine = nc.vector if s == 0 and t < 3 else nc.gpsimd
-                engine.memset(cells[s][t][:], 0.0)
+                nc.vector.memset(cells[s][t][:].bitcast(I32), 0)
 
-        def deal_views(s):
-            dst = w_dealt[s][:].rearrange("p (t m j) -> p m j t", t=PACK, j=PACK)
-            src = w_raw[s][:].rearrange("p j (m t) -> p m j t", t=PACK)
+        def deal_views(s, raw, m0):
+            src = raw[:].rearrange("p j (m t) -> p m j t", t=PACK)
+            dst = w_dealt[s][:].rearrange("p (t m j) -> p m j t", t=PACK, j=PACK)[:, m0 : m0 + src.shape[1], :, :]
             return dst, src
 
         def picked(table, s):
@@ -108,6 +110,8 @@ def tile_picked_bev_max_po_kernel(
 
         def first_products(s):
             banks = []
+            for half in range(2):
+                hidden_pair(s, half)
             for t in range(PACK):
                 bank = psum.tile([P, V], F32, name="bank")
                 cols = slice(t * P, (t + 1) * P)
@@ -123,21 +127,31 @@ def tile_picked_bev_max_po_kernel(
                 banks.append(bank)
             return banks
 
+        def hidden_pair(s, half):
+            tag = {(0, 0): "w2_raw0", (0, 1): "w3_raw"}.get((s, half), "hidden%d%d" % (s, half))
+            pair = keep.tile([P, 2, V], F32, name="hidden%d%d" % (s, half), tag=tag, align_bytes=64)
+            for u in range(2):
+                hidden[(s, 2 * half + u)] = pair[:, u, :]
+
+        def gather_bytes(s):
+            picked_bytes.append(keep.tile([P, V], U8, name="picked_bytes%d" % s, tag="picked_bytes", align_bytes=64))
+            nc.vector.tensor_copy(out=picked_bytes[s][:], in_=picked(x_bytes[:], s))
+
         def relu_scalar(s, t, bank):
-            nc.scalar.activation(out=hidden[s][t][:], in_=bank[:], func=ACT.Relu)
+            nc.scalar.activation(out=hidden[(s, t)], in_=bank[:], func=ACT.Relu)
 
         def relu_vector(s, t, bank):
-            nc.vector.tensor_scalar_max(out=hidden[s][t][:], in0=bank[:], scalar1=0.0)
+            nc.vector.tensor_scalar_max(out=hidden[(s, t)], in0=bank[:], scalar1=0.0)
 
         def scatter_vector(s, t, lo, hi):
             window = cells[s][t][:].indirect(lists[s][:, lo // LANE : hi // LANE])
-            nc.vector.tensor_copy(out=window, in_=hidden[s][t][:, lo:hi])
+            nc.vector.tensor_copy(out=window, in_=hidden[(s, t)][:, lo:hi])
 
         def scatter_scalar(s, t, lo, hi):
-            for a in range(lo, hi, 384 if hi - lo == 384 else HALF):
-                b = min(hi, a + (384 if hi - lo == 384 else HALF))
-                window = cells[s][t][:].indirect(lists[s][:, a // LANE : b // LANE])
-                nc.scalar.activation(out=window, in_=hidden[s][t][:, a:b], func=ACT.Copy)
+            step = hi - lo if hi - lo <= 384 else HALF
+            for a in range(lo, hi, step):
+                window = cells[s][t][:].indirect(lists[s][:, a // LANE : (a + step) // LANE])
+                nc.scalar.activation(out=window, in_=hidden[(s, t)][:, a : a + step], func=ACT.Copy)
 
         def join(t, lo, hi):
             nc.vector.tensor_tensor(
@@ -147,28 +161,30 @@ def tile_picked_bev_max_po_kernel(
                 op=ALU.max,
             )
 
-        dst, src = deal_views(0)
+        dst, src = deal_views(0, w1_raw, 0)
         nc.scalar.activation(out=dst, in_=src, func=ACT.Copy)
-        nc.vector.tensor_copy(out=picked_bytes[0][:], in_=picked(x_bytes[:], 0))
+        dst, src = deal_views(1, w2_raw[0], 0)
+        nc.scalar.activation(out=dst, in_=src, func=ACT.Copy)
+        nc.scalar.copy(
+            out=w3_codes[:].rearrange("p (t m) -> p m t", t=PACK),
+            in_=w3_raw[:].bitcast(U32).rearrange("p (m t) -> p m t", t=PACK),
+        )
+        gather_bytes(0)
         quantize(w_codes[0][:], w_scales[0][:], w_dealt[0][:])
         nc.vector.tensor_copy(out=picked_words[0][:], in_=picked(x_table[:].bitcast(U32), 0))
         banks = first_products(0)
         for t in range(PACK):
             relu_scalar(0, t, banks[t])
         nc.vector.tensor_copy(out=picked_words[1][:], in_=picked(x_table[:].bitcast(U32), 1))
-        nc.vector.tensor_copy(out=picked_bytes[1][:], in_=picked(x_bytes[:], 1))
+        gather_bytes(1)
         scatter_vector(0, 0, 0, V)
         scatter_vector(0, 3, 0, SHARE)
         scatter_scalar(0, 1, 0, V)
         scatter_scalar(0, 2, 0, V)
         scatter_scalar(0, 3, SHARE, V)
 
-        dst, src = deal_views(1)
+        dst, src = deal_views(1, w2_raw[1], P // 2)
         nc.vector.tensor_copy(out=dst, in_=src)
-        nc.vector.tensor_copy(
-            out=w3_codes[:].rearrange("p (t m) -> p m t", t=PACK),
-            in_=w3_raw[:].bitcast(U32).rearrange("p (m t) -> p m t", t=PACK),
-        )
         quantize(w_codes[1][:], w_scales[1][:], w_dealt[1][:])
         nc.vector.tensor_copy(
             out=w3_bytes[:].rearrange("p (t m) -> p m t", t=PACK),

@@ -19,15 +19,17 @@ P = 128
 PACK = 4
 QUADS = 4
 LANE = 16
+BANK = 512
+BANKS = 8
 UNIT = 128
-UNITS = U // UNIT
-WIDTHS = [128,256,256,256,128]
+WIDTHS = [128, 256, 256, 256, 128]
 CHUNKS = len(WIDTHS)
 STARTS = [sum(WIDTHS[:c]) for c in range(CHUNKS)]
-BANK = 512
+WORDS_EARLY = STARTS[3]
 RUN = 4
 HALF = 256
 SHARE = 192
+NEAR, FAR = 0, 1
 
 
 def tile_picked_bev_max_po_kernel(
@@ -36,10 +38,13 @@ def tile_picked_bev_max_po_kernel(
     nc = tc.nc
     with ExitStack() as ctx:
         keep = ctx.enter_context(tc.tile_pool(name="keep", bufs=1))
-        psum = ctx.enter_context(tc.psum_pool(name="psum", bufs=8))
+        psum = ctx.enter_context(tc.psum_pool(name="psum", bufs=BANKS))
 
         def tiles(name, count, shape, dtype):
             return [keep.tile(shape, dtype, name="%s%d" % (name, i), align_bytes=64) for i in range(count)]
+
+        def chunk_tiles(name, shape, dtype):
+            return [keep.tile(shape(w), dtype, name="%s%d" % (name, c), align_bytes=64) for c, w in enumerate(WIDTHS)]
 
         offs_t = keep.tile([P, S // LANE], U16)
         near_t = keep.tile([P, V // LANE], U16)
@@ -49,7 +54,9 @@ def tile_picked_bev_max_po_kernel(
         x_table = keep.tile([P, T], I32, align_bytes=64)
         x_bytes = keep.tile([P, T], U8, align_bytes=64)
         w1_raw = keep.tile([P, PACK, H], F32, align_bytes=64)
-        w2_raw = [keep.tile([P, PACK, H // 2], F32, name="w2_raw%d" % i, tag="w2_raw%d" % i, align_bytes=64) for i in range(2)]
+        w2_raw = [
+            keep.tile([P, PACK, H // 2], F32, name="w2_raw%d" % i, tag="w2_raw%d" % i, align_bytes=64) for i in range(2)
+        ]
         w_dealt = tiles("w_dealt", 2, [P, H * PACK], BF16)
         w_codes = tiles("w_codes", 2, [P, H], U32)
         w_scales = tiles("w_scales", 2, [P, H], U8)
@@ -61,11 +68,7 @@ def tile_picked_bev_max_po_kernel(
         picked_bytes = []
         hidden = {}
         cells = [tiles("cells%d_" % s, PACK, [P, U], F32) for s in range(2)]
-        z_rows = keep.tile([P, UNITS, PACK, UNIT], BF16, align_bytes=64)
-
-        def chunk_tiles(name, shape, dtype):
-            return [keep.tile(shape(w), dtype, name="%s%d" % (name, c), align_bytes=64) for c, w in enumerate(WIDTHS)]
-
+        z_rows = keep.tile([P, U // UNIT, PACK, UNIT], BF16, align_bytes=64)
         z_woven = chunk_tiles("z_woven", lambda w: [P, w, PACK], BF16)
         z_codes = chunk_tiles("z_codes", lambda w: [P, w], U32)
         z_scales = chunk_tiles("z_scales", lambda w: [P, w], U8)
@@ -74,15 +77,17 @@ def tile_picked_bev_max_po_kernel(
         y_codes = keep.tile([P, U], U32, align_bytes=64)
         y_scales = keep.tile([P, U], U8, align_bytes=64)
 
-        def load_scale_rows(queue, plane, rows):
+        def load_scale_rows(plane, rows):
             for q in range(QUADS):
-                queue.dma_start(out=plane[32 * q : 32 * q + 4, :].bitcast(I32), in_=rows[4 * q : 4 * q + 4, :].bitcast(I32))
+                nc.sync.dma_start(
+                    out=plane[32 * q : 32 * q + 4, :].bitcast(I32), in_=rows[4 * q : 4 * q + 4, :].bitcast(I32)
+                )
 
         nc.vector.memset(x_bytes[:].bitcast(I32), 0)
         nc.vector.memset(w3_raw_bytes[:].bitcast(I32), 0)
 
         nc.sync.dma_start(out=w1_raw[:], in_=w1.rearrange("(p j) c -> p j c", j=PACK))
-        load_scale_rows(nc.sync, x_bytes, x_scales[0])
+        load_scale_rows(x_bytes, x_scales[0])
         nc.sync.dma_start(offs_t[:], offs)
         nc.sync.dma_start(out=x_table[:], in_=x_words[0].rearrange("p n r -> p (n r)").bitcast(I32))
         nc.sync.dma_start(near_t[:], near)
@@ -91,7 +96,7 @@ def tile_picked_bev_max_po_kernel(
         nc.sync.dma_start(out=w3_raw[:], in_=w3_words[0].rearrange("p n r -> p (n r)").bitcast(I32))
         nc.sync.dma_start(out=w2_raw[1][:], in_=w2_rows[:, :, H // 2 :])
         nc.sync.dma_start(far_t[:], far)
-        load_scale_rows(nc.sync, w3_raw_bytes, w3_scales[0])
+        load_scale_rows(w3_raw_bytes, w3_scales[0])
 
         for s in range(2):
             for t in range(PACK):
@@ -105,13 +110,28 @@ def tile_picked_bev_max_po_kernel(
         def picked(table, s):
             return table.indirect(offs_t[:, s * V // LANE : (s + 1) * V // LANE])
 
+        def gather_words(s):
+            nc.vector.tensor_copy(out=picked_words[s][:], in_=picked(x_table[:].bitcast(U32), s))
+
+        def gather_bytes(s):
+            tag = "picked_bytes" if s == NEAR else "w2_raw0"
+            picked_bytes.append(keep.tile([P, V], U8, name="picked_bytes%d" % s, tag=tag, align_bytes=64))
+            nc.vector.tensor_copy(out=picked_bytes[s][:], in_=picked(x_bytes[:], s))
+
         def quantize(codes, scales, values):
             nc.vector.quantize_mx(out=codes.bitcast(FP8X4), scales=scales, in_=values)
 
+        def hidden_tiles(s):
+            tags = ("w2_raw0", "w3_raw") if s == NEAR else ("far_first", "far_rest")
+            first = keep.tile([P, V], F32, name="hidden_first%d" % s, tag=tags[0], align_bytes=64)
+            rest = keep.tile([P, PACK - 1, V], F32, name="hidden_rest%d" % s, tag=tags[1], align_bytes=64)
+            hidden[(s, 0)] = first[:]
+            for t in range(1, PACK):
+                hidden[(s, t)] = rest[:, t - 1, :]
+
         def first_products(s):
             banks = []
-            for half in range(2):
-                hidden_pair(s, half)
+            hidden_tiles(s)
             for t in range(PACK):
                 bank = psum.tile([P, V], F32, name="bank")
                 cols = slice(t * P, (t + 1) * P)
@@ -127,16 +147,6 @@ def tile_picked_bev_max_po_kernel(
                 banks.append(bank)
             return banks
 
-        def hidden_pair(s, half):
-            tag = {(0, 0): "w2_raw0", (0, 1): "w3_raw"}.get((s, half), "hidden%d%d" % (s, half))
-            pair = keep.tile([P, 2, V], F32, name="hidden%d%d" % (s, half), tag=tag, align_bytes=64)
-            for u in range(2):
-                hidden[(s, 2 * half + u)] = pair[:, u, :]
-
-        def gather_bytes(s):
-            picked_bytes.append(keep.tile([P, V], U8, name="picked_bytes%d" % s, tag="picked_bytes", align_bytes=64))
-            nc.vector.tensor_copy(out=picked_bytes[s][:], in_=picked(x_bytes[:], s))
-
         def relu_scalar(s, t, bank):
             nc.scalar.activation(out=hidden[(s, t)], in_=bank[:], func=ACT.Relu)
 
@@ -148,63 +158,65 @@ def tile_picked_bev_max_po_kernel(
             nc.vector.tensor_copy(out=window, in_=hidden[(s, t)][:, lo:hi])
 
         def scatter_scalar(s, t, lo, hi):
-            step = hi - lo if hi - lo <= 384 else HALF
-            for a in range(lo, hi, step):
-                window = cells[s][t][:].indirect(lists[s][:, a // LANE : (a + step) // LANE])
-                nc.scalar.activation(out=window, in_=hidden[(s, t)][:, a : a + step], func=ACT.Copy)
+            window = cells[s][t][:].indirect(lists[s][:, lo // LANE : hi // LANE])
+            nc.scalar.activation(out=window, in_=hidden[(s, t)][:, lo:hi], func=ACT.Copy)
 
         def join(t, lo, hi):
             nc.vector.tensor_tensor(
                 out=z_rows[:, lo // UNIT : hi // UNIT, t, :],
-                in0=cells[0][t][:, lo:hi].rearrange("p (u c) -> p u c", c=UNIT),
-                in1=cells[1][t][:, lo:hi].rearrange("p (u c) -> p u c", c=UNIT),
+                in0=cells[NEAR][t][:, lo:hi].rearrange("p (u c) -> p u c", c=UNIT),
+                in1=cells[FAR][t][:, lo:hi].rearrange("p (u c) -> p u c", c=UNIT),
                 op=ALU.max,
             )
 
-        dst, src = deal_views(0, w1_raw, 0)
+        dst, src = deal_views(NEAR, w1_raw, 0)
         nc.scalar.activation(out=dst, in_=src, func=ACT.Copy)
-        dst, src = deal_views(1, w2_raw[0], 0)
+        dst, src = deal_views(FAR, w2_raw[0], 0)
         nc.scalar.activation(out=dst, in_=src, func=ACT.Copy)
         nc.scalar.copy(
             out=w3_codes[:].rearrange("p (t m) -> p m t", t=PACK),
             in_=w3_raw[:].bitcast(U32).rearrange("p (m t) -> p m t", t=PACK),
         )
-        gather_bytes(0)
-        quantize(w_codes[0][:], w_scales[0][:], w_dealt[0][:])
-        nc.vector.tensor_copy(out=picked_words[0][:], in_=picked(x_table[:].bitcast(U32), 0))
-        banks = first_products(0)
+        gather_bytes(NEAR)
+        quantize(w_codes[NEAR][:], w_scales[NEAR][:], w_dealt[NEAR][:])
+        gather_words(NEAR)
+        banks = first_products(NEAR)
         for t in range(PACK):
-            relu_scalar(0, t, banks[t])
-        nc.vector.tensor_copy(out=picked_words[1][:], in_=picked(x_table[:].bitcast(U32), 1))
-        gather_bytes(1)
-        scatter_vector(0, 0, 0, V)
-        scatter_vector(0, 3, 0, SHARE)
-        scatter_scalar(0, 1, 0, V)
-        scatter_scalar(0, 2, 0, V)
-        scatter_scalar(0, 3, SHARE, V)
+            relu_scalar(NEAR, t, banks[t])
+        gather_words(FAR)
+        scatter_vector(NEAR, 0, 0, V)
+        gather_bytes(FAR)
+        scatter_vector(NEAR, 3, 0, SHARE)
+        for lo in range(0, V, HALF):
+            for t in (1, 2):
+                scatter_scalar(NEAR, t, lo, lo + HALF)
+        scatter_scalar(NEAR, 3, SHARE, V)
 
-        dst, src = deal_views(1, w2_raw[1], P // 2)
+        dst, src = deal_views(FAR, w2_raw[1], P // 2)
         nc.vector.tensor_copy(out=dst, in_=src)
-        quantize(w_codes[1][:], w_scales[1][:], w_dealt[1][:])
         nc.vector.tensor_copy(
             out=w3_bytes[:].rearrange("p (t m) -> p m t", t=PACK),
             in_=w3_raw_bytes[:].rearrange("p (m t) -> p m t", t=PACK),
         )
-        banks = first_products(1)
-        for t in range(2):
-            relu_vector(1, t, banks[t])
-            scatter_vector(1, t, 0, V)
+        quantize(w_codes[FAR][:], w_scales[FAR][:], w_dealt[FAR][:])
+        banks = first_products(FAR)
+        for t in (0, 1):
+            relu_vector(FAR, t, banks[t])
+        for t in (2, 3):
+            relu_scalar(FAR, t, banks[t])
+        for t in (0, 1):
+            scatter_vector(FAR, t, 0, V)
+        for lo in range(0, V, HALF):
+            for t in (2, 3):
+                scatter_scalar(FAR, t, lo, lo + HALF)
+        for t in range(PACK - 1):
             join(t, 0, U)
-        for t in range(2, PACK):
-            relu_scalar(1, t, banks[t])
-            scatter_scalar(1, t, 0, V)
-        join(2, 0, U)
 
         out_rows = out_0.rearrange("(p t) r -> p t r", t=PACK)
         out_words = out_1[0].rearrange("p n r -> p (n r)").bitcast(I32)
 
-        def z_join(c):
-            join(3, STARTS[c], STARTS[c] + WIDTHS[c])
+        def last_join(c):
+            join(PACK - 1, STARTS[c], STARTS[c] + WIDTHS[c])
 
         def z_weave(c, copy):
             rows = z_rows[:, STARTS[c] // UNIT : (STARTS[c] + WIDTHS[c]) // UNIT, :, :]
@@ -247,34 +259,37 @@ def tile_picked_bev_max_po_kernel(
         def store_words(lo, hi):
             nc.sync.dma_start(out=out_words[:, lo:hi], in_=y_codes[:, lo:hi].bitcast(I32))
 
-        z_join(0)
-        z_weave(0, nc.vector.tensor_copy)
-        z_join(1)
-        z_weave(1, nc.scalar.copy)
+        on_vector, on_scalar = nc.vector.tensor_copy, nc.scalar.copy
+        last_join(0)
+        z_weave(0, on_vector)
+        last_join(1)
+        z_weave(1, on_scalar)
         z_product(0)
-        y_weave(0, nc.scalar.copy)
-        z_join(2)
-        z_weave(2, nc.vector.tensor_copy)
-        z_join(3)
+        y_weave(0, on_scalar)
+        last_join(2)
+        z_weave(2, on_vector)
+        last_join(3)
         z_product(1)
         z_product(2)
-        z_weave(3, nc.vector.tensor_copy)
-        z_join(4)
+        z_weave(3, on_vector)
+        last_join(4)
         z_product(3)
-        z_weave(4, nc.vector.tensor_copy)
+        z_weave(4, on_vector)
         y_planes(0)
         z_product(4)
-        y_weave(1, nc.vector.tensor_copy)
-        y_weave(2, nc.vector.tensor_copy)
+        y_weave(1, on_vector)
+        y_weave(2, on_vector)
         y_planes(1)
-        y_weave(3, nc.vector.tensor_copy)
+        y_weave(3, on_vector)
         y_planes(2)
-        store_words(0, 640)
-        y_weave(4, nc.scalar.copy)
+        store_words(0, WORDS_EARLY)
+        y_weave(4, on_scalar)
         y_planes(3)
         y_planes(4)
-        store_words(640, U)
+        store_words(WORDS_EARLY, U)
 
         for q in range(QUADS):
             queue = nc.scalar if q % 2 else nc.sync
-            queue.dma_start(out=out_2[0][4 * q : 4 * q + 4, :].bitcast(I32), in_=y_scales[32 * q : 32 * q + 4, :].bitcast(I32))
+            queue.dma_start(
+                out=out_2[0][4 * q : 4 * q + 4, :].bitcast(I32), in_=y_scales[32 * q : 32 * q + 4, :].bitcast(I32)
+            )

from contextlib import ExitStack

import concourse.mybir as mybir

K, T, S, H, U, V = 512, 2048, 1024, 512, 1024, 512
FLOPS = 2 * K * H * S + 2 * H * H * U

F32 = mybir.dt.float32
BF16 = mybir.dt.bfloat16
I32 = mybir.dt.int32
U32 = mybir.dt.uint32
U16 = mybir.dt.uint16
U8 = mybir.dt.uint8
FP8X4 = mybir.dt.float8_e4m3fn_x4
ACT = mybir.ActivationFunctionType
ALU = mybir.AluOpType

P = 128
PACK = 4
QUADS = 4
LANE = 16
BANK = 512
BANKS = 8
UNIT = 128
WIDTHS = [128, 256, 256, 256, 128]
CHUNKS = len(WIDTHS)
STARTS = [sum(WIDTHS[:c]) for c in range(CHUNKS)]
WORDS_EARLY = STARTS[3]
RUN = 4
HALF = 256
SHARE = 192
NEAR, FAR = 0, 1


def tile_picked_bev_max_po_kernel(
    tc, x_words, x_scales, w1, w2, w3_words, w3_scales, offs, near, far, out_0, out_1, out_2
):
    nc = tc.nc
    with ExitStack() as ctx:
        keep = ctx.enter_context(tc.tile_pool(name="keep", bufs=1))
        psum = ctx.enter_context(tc.psum_pool(name="psum", bufs=BANKS))

        def tiles(name, count, shape, dtype):
            return [keep.tile(shape, dtype, name="%s%d" % (name, i), align_bytes=64) for i in range(count)]

        def chunk_tiles(name, shape, dtype):
            return [keep.tile(shape(w), dtype, name="%s%d" % (name, c), align_bytes=64) for c, w in enumerate(WIDTHS)]

        offs_t = keep.tile([P, S // LANE], U16)
        near_t = keep.tile([P, V // LANE], U16)
        far_t = keep.tile([P, V // LANE], U16)
        lists = [near_t, far_t]

        x_table = keep.tile([P, T], I32, align_bytes=64)
        x_bytes = keep.tile([P, T], U8, align_bytes=64)
        w1_raw = keep.tile([P, PACK, H], F32, align_bytes=64)
        w2_raw = [
            keep.tile([P, PACK, H // 2], F32, name="w2_raw%d" % i, tag="w2_raw%d" % i, align_bytes=64) for i in range(2)
        ]
        w_dealt = tiles("w_dealt", 2, [P, H * PACK], BF16)
        w_codes = tiles("w_codes", 2, [P, H], U32)
        w_scales = tiles("w_scales", 2, [P, H], U8)
        w3_raw = keep.tile([P, H], I32, tag="w3_raw", align_bytes=64)
        w3_raw_bytes = keep.tile([P, H], U8, align_bytes=64)
        w3_codes = keep.tile([P, H], U32, align_bytes=64)
        w3_bytes = keep.tile([P, H], U8, align_bytes=64)
        picked_words = tiles("picked_words", 2, [P, V], U32)
        picked_bytes = []
        hidden = {}
        cells = [tiles("cells%d_" % s, PACK, [P, U], F32) for s in range(2)]
        z_rows = keep.tile([P, U // UNIT, PACK, UNIT], BF16, align_bytes=64)
        z_woven = chunk_tiles("z_woven", lambda w: [P, w, PACK], BF16)
        z_codes = chunk_tiles("z_codes", lambda w: [P, w], U32)
        z_scales = chunk_tiles("z_scales", lambda w: [P, w], U8)
        y_rows = chunk_tiles("y_rows", lambda w: [P, PACK, w], F32)
        y_woven = chunk_tiles("y_woven", lambda w: [P, w, PACK], BF16)
        y_codes = keep.tile([P, U], U32, align_bytes=64)
        y_scales = keep.tile([P, U], U8, align_bytes=64)

        def load_scale_rows(plane, rows):
            for q in range(QUADS):
                nc.sync.dma_start(
                    out=plane[32 * q : 32 * q + 4, :].bitcast(I32), in_=rows[4 * q : 4 * q + 4, :].bitcast(I32)
                )

        nc.vector.memset(x_bytes[:].bitcast(I32), 0)
        nc.vector.memset(w3_raw_bytes[:].bitcast(I32), 0)

        nc.sync.dma_start(out=w1_raw[:], in_=w1.rearrange("(p j) c -> p j c", j=PACK))
        load_scale_rows(x_bytes, x_scales[0])
        nc.sync.dma_start(offs_t[:], offs)
        nc.sync.dma_start(out=x_table[:], in_=x_words[0].rearrange("p n r -> p (n r)").bitcast(I32))
        nc.sync.dma_start(near_t[:], near)
        w2_rows = w2.rearrange("(p j) c -> p j c", j=PACK)
        nc.sync.dma_start(out=w2_raw[0][:], in_=w2_rows[:, :, : H // 2])
        nc.sync.dma_start(out=w3_raw[:], in_=w3_words[0].rearrange("p n r -> p (n r)").bitcast(I32))
        nc.sync.dma_start(out=w2_raw[1][:], in_=w2_rows[:, :, H // 2 :])
        nc.sync.dma_start(far_t[:], far)
        load_scale_rows(w3_raw_bytes, w3_scales[0])

        for s in range(2):
            for t in range(PACK):
                nc.vector.memset(cells[s][t][:].bitcast(I32), 0)

        def deal_views(s, raw, m0):
            src = raw[:].rearrange("p j (m t) -> p m j t", t=PACK)
            dst = w_dealt[s][:].rearrange("p (t m j) -> p m j t", t=PACK, j=PACK)[:, m0 : m0 + src.shape[1], :, :]
            return dst, src

        def picked(table, s):
            return table.indirect(offs_t[:, s * V // LANE : (s + 1) * V // LANE])

        def gather_words(s):
            nc.vector.tensor_copy(out=picked_words[s][:], in_=picked(x_table[:].bitcast(U32), s))

        def gather_bytes(s):
            tag = "picked_bytes" if s == NEAR else "w2_raw0"
            picked_bytes.append(keep.tile([P, V], U8, name="picked_bytes%d" % s, tag=tag, align_bytes=64))
            nc.vector.tensor_copy(out=picked_bytes[s][:], in_=picked(x_bytes[:], s))

        def quantize(codes, scales, values):
            nc.vector.quantize_mx(out=codes.bitcast(FP8X4), scales=scales, in_=values)

        def hidden_tiles(s):
            tags = ("w2_raw0", "w3_raw") if s == NEAR else ("far_first", "far_rest")
            first = keep.tile([P, V], F32, name="hidden_first%d" % s, tag=tags[0], align_bytes=64)
            rest = keep.tile([P, PACK - 1, V], F32, name="hidden_rest%d" % s, tag=tags[1], align_bytes=64)
            hidden[(s, 0)] = first[:]
            for t in range(1, PACK):
                hidden[(s, t)] = rest[:, t - 1, :]

        def first_products(s):
            banks = []
            hidden_tiles(s)
            for t in range(PACK):
                bank = psum.tile([P, V], F32, name="bank")
                cols = slice(t * P, (t + 1) * P)
                nc.tensor.matmul_mx(
                    out=bank[:],
                    lhsT=w_codes[s][:, cols].bitcast(FP8X4),
                    lhsT_scale=w_scales[s][:, cols],
                    rhs=picked_words[s][:].bitcast(FP8X4),
                    rhs_scale=picked_bytes[s][:],
                    start=True,
                    stop=True,
                )
                banks.append(bank)
            return banks

        def relu_scalar(s, t, bank):
            nc.scalar.activation(out=hidden[(s, t)], in_=bank[:], func=ACT.Relu)

        def relu_vector(s, t, bank):
            nc.vector.tensor_scalar_max(out=hidden[(s, t)], in0=bank[:], scalar1=0.0)

        def scatter_vector(s, t, lo, hi):
            window = cells[s][t][:].indirect(lists[s][:, lo // LANE : hi // LANE])
            nc.vector.tensor_copy(out=window, in_=hidden[(s, t)][:, lo:hi])

        def scatter_scalar(s, t, lo, hi):
            window = cells[s][t][:].indirect(lists[s][:, lo // LANE : hi // LANE])
            nc.scalar.activation(out=window, in_=hidden[(s, t)][:, lo:hi], func=ACT.Copy)

        def join(t, lo, hi):
            nc.vector.tensor_tensor(
                out=z_rows[:, lo // UNIT : hi // UNIT, t, :],
                in0=cells[NEAR][t][:, lo:hi].rearrange("p (u c) -> p u c", c=UNIT),
                in1=cells[FAR][t][:, lo:hi].rearrange("p (u c) -> p u c", c=UNIT),
                op=ALU.max,
            )

        dst, src = deal_views(NEAR, w1_raw, 0)
        nc.scalar.activation(out=dst, in_=src, func=ACT.Copy)
        dst, src = deal_views(FAR, w2_raw[0], 0)
        nc.scalar.activation(out=dst, in_=src, func=ACT.Copy)
        nc.scalar.copy(
            out=w3_codes[:].rearrange("p (t m) -> p m t", t=PACK),
            in_=w3_raw[:].bitcast(U32).rearrange("p (m t) -> p m t", t=PACK),
        )
        gather_bytes(NEAR)
        quantize(w_codes[NEAR][:], w_scales[NEAR][:], w_dealt[NEAR][:])
        gather_words(NEAR)
        banks = first_products(NEAR)
        for t in range(PACK):
            relu_scalar(NEAR, t, banks[t])
        gather_words(FAR)
        scatter_vector(NEAR, 0, 0, V)
        gather_bytes(FAR)
        scatter_vector(NEAR, 3, 0, SHARE)
        for lo in range(0, V, HALF):
            for t in (1, 2):
                scatter_scalar(NEAR, t, lo, lo + HALF)
        scatter_scalar(NEAR, 3, SHARE, V)

        dst, src = deal_views(FAR, w2_raw[1], P // 2)
        nc.vector.tensor_copy(out=dst, in_=src)
        nc.vector.tensor_copy(
            out=w3_bytes[:].rearrange("p (t m) -> p m t", t=PACK),
            in_=w3_raw_bytes[:].rearrange("p (m t) -> p m t", t=PACK),
        )
        quantize(w_codes[FAR][:], w_scales[FAR][:], w_dealt[FAR][:])
        banks = first_products(FAR)
        for t in (0, 1):
            relu_vector(FAR, t, banks[t])
        for t in (2, 3):
            relu_scalar(FAR, t, banks[t])
        for t in (0, 1):
            scatter_vector(FAR, t, 0, V)
        for lo in range(0, V, HALF):
            for t in (2, 3):
                scatter_scalar(FAR, t, lo, lo + HALF)
        for t in range(PACK - 1):
            join(t, 0, U)

        out_rows = out_0.rearrange("(p t) r -> p t r", t=PACK)
        out_words = out_1[0].rearrange("p n r -> p (n r)").bitcast(I32)

        def last_join(c):
            join(PACK - 1, STARTS[c], STARTS[c] + WIDTHS[c])

        def z_weave(c, copy):
            rows = z_rows[:, STARTS[c] // UNIT : (STARTS[c] + WIDTHS[c]) // UNIT, :, :]
            copy(
                out=z_woven[c][:].rearrange("p (u c i) t -> p u c t i", c=UNIT // RUN, i=RUN),
                in_=rows.rearrange("p u t (c i) -> p u c t i", i=RUN),
            )

        def z_product(c):
            width = WIDTHS[c]
            cols = slice(STARTS[c], STARTS[c] + width)
            quantize(z_codes[c][:], z_scales[c][:], z_woven[c][:].rearrange("p c t -> p (c t)"))
            per_bank = BANK // width
            for t0 in range(0, PACK, per_bank):
                bank = psum.tile([P, per_bank, width], F32, name="bank")
                for u in range(per_bank):
                    rows = slice((t0 + u) * P, (t0 + u + 1) * P)
                    nc.tensor.matmul_mx(
                        out=bank[:, u, :],
                        lhsT=w3_codes[:, rows].bitcast(FP8X4),
                        lhsT_scale=w3_bytes[:, rows],
                        rhs=z_codes[c][:].bitcast(FP8X4),
                        rhs_scale=z_scales[c][:],
                        start=True,
                        stop=True,
                    )
                nc.scalar.copy(out=y_rows[c][:, t0 : t0 + per_bank, :], in_=bank[:])
            nc.sync.dma_start(out=out_rows[:, :, cols], in_=y_rows[c][:])

        def y_weave(c, copy):
            copy(
                out=y_woven[c][:].rearrange("p (c i) t -> p c t i", i=RUN),
                in_=y_rows[c][:].rearrange("p t (c i) -> p c t i", i=RUN),
            )

        def y_planes(c):
            cols = slice(STARTS[c], STARTS[c] + WIDTHS[c])
            quantize(y_codes[:, cols], y_scales[:, cols], y_woven[c][:].rearrange("p c t -> p (c t)"))

        def store_words(lo, hi):
            nc.sync.dma_start(out=out_words[:, lo:hi], in_=y_codes[:, lo:hi].bitcast(I32))

        on_vector, on_scalar = nc.vector.tensor_copy, nc.scalar.copy
        last_join(0)
        z_weave(0, on_vector)
        last_join(1)
        z_weave(1, on_scalar)
        z_product(0)
        y_weave(0, on_scalar)
        last_join(2)
        z_weave(2, on_vector)
        last_join(3)
        z_product(1)
        z_product(2)
        z_weave(3, on_vector)
        last_join(4)
        z_product(3)
        z_weave(4, on_vector)
        y_planes(0)
        z_product(4)
        y_weave(1, on_vector)
        y_weave(2, on_vector)
        y_planes(1)
        y_weave(3, on_vector)
        y_planes(2)
        store_words(0, WORDS_EARLY)
        y_weave(4, on_scalar)
        y_planes(3)
        y_planes(4)
        store_words(WORDS_EARLY, U)

        for q in range(QUADS):
            queue = nc.scalar if q % 2 else nc.sync
            queue.dma_start(
                out=out_2[0][4 * q : 4 * q + 4, :].bitcast(I32), in_=y_scales[32 * q : 32 * q + 4, :].bitcast(I32)
            )
